import numpy as np
import ml_dtypes


def mxq(x, axis, fmt="e4m3"):
    dtype, down = {"e4m3": (ml_dtypes.float8_e4m3fn, 7), "e5m2": (ml_dtypes.float8_e5m2, 14)}[fmt]
    v = np.moveaxis(np.asarray(x, np.float32).astype(ml_dtypes.bfloat16).astype(np.float64), axis, -1)
    blocks = v.reshape(v.shape[:-1] + (-1, 32))
    amax = np.abs(blocks).max(-1, keepdims=True)
    byte = np.maximum(np.where(amax > 0, np.frexp(amax)[1] - 1 + 127, 0) - down, 1)
    scale = np.exp2(byte - 127.0)
    codes = (blocks / scale).astype(np.float32).astype(dtype).astype(np.float64)
    return np.moveaxis((codes * scale).reshape(v.shape), -1, axis)


WIDE = False


def mx_kscale(k):
    if not WIDE:
        return np.ones(k)
    levels = np.array([24, -24, 12, -12, 0])
    if k % 512:
        return np.exp2(np.random.permutation(np.resize(levels, k // 32))).repeat(32)
    a = np.empty((k // 512, 16))
    for p in range(k // 512):
        a[p, :8] = np.random.permutation(np.resize(levels, 8))
        for g in range(8):
            far = levels[np.abs(levels - a[p, g]) >= 10]
            a[p, g + 8] = far[np.random.randint(len(far))]
    return np.exp2(a.ravel()).repeat(32)


def f64(x):
    return np.asarray(x).astype(np.float64)


def striped(idx):
    return np.tile(idx.reshape(-1, 16).T, (8, 1)).astype(np.uint16)


def unstriped(offs):
    return offs[:16].T.reshape(-1).astype(np.int64)


E2M1 = np.array([0.0, 0.5, 1.0, 1.5, 2.0, 3.0, 4.0, 6.0, -0.0, -0.5, -1.0, -1.5, -2.0, -3.0, -4.0, -6.0])


def pack_weight(w, fmt):
    k, n = w.shape
    w = f64(np.asarray(w, np.float32).astype(ml_dtypes.bfloat16)).reshape(k // 32, 32, n)
    amax = np.abs(w).max(1)
    if fmt == "e4m3":
        byte = np.frexp(amax)[1] - 1 + 127 - 7
    else:
        mant, ex = np.frexp(amax / 6.0)
        byte = np.where(mant > 0.5, ex, ex - 1) + 127
    byte = np.clip(np.where(amax > 0, byte, 1), 1, 254)
    scaled = (w * np.exp2(127.0 - byte)[:, None, :]).reshape(k, n).astype(np.float32)
    by_word = np.ascontiguousarray(scaled.reshape(k // 512, 128, 4, n).transpose(0, 1, 3, 2))
    if fmt == "e4m3":
        words = by_word.astype(ml_dtypes.float8_e4m3fn).view(np.uint8)
    else:
        c = by_word.astype(ml_dtypes.float4_e2m1fn).view(np.uint8) & 0xF
        words = (c[..., 0::2] | (c[..., 1::2] << 4)).reshape(k // 512, 128, 2 * n)
    return np.ascontiguousarray(words), np.ascontiguousarray(byte.astype(np.uint8).reshape(k // 512, 16, n))


def unpack_weight(words, scales, fmt):
    g, _, n = scales.shape
    words = np.ascontiguousarray(words).reshape(g, 128, n, -1)
    if fmt == "e4m3":
        vals = words.view(ml_dtypes.float8_e4m3fn).astype(np.float64)
    else:
        nib = np.empty((g, 128, n, 4), np.uint8)
        nib[..., 0::2] = words & 0xF
        nib[..., 1::2] = words >> 4
        vals = E2M1[nib]
    vals = vals * np.repeat(np.exp2(scales.astype(np.float64) - 127.0), 8, axis=1)[..., None]
    return vals.transpose(0, 1, 3, 2).reshape(g * 512, n)


def sigm(f):
    return 1.0 / (1.0 + np.exp(-np.maximum(f, -700.0)))


K, N, T, J = 1024, 512, 4096, 1024


def setup_inputs():
    n = np.random.standard_normal
    s = mx_kscale(K)[:, None]
    wv = n((K, N)) / np.sqrt(K) / s
    p_tab = pack_weight(n((K, T)) * s, "e4m3")
    p_wk = pack_weight(n((K, N)) / np.sqrt(K) / s, "e4m3")
    p_wv4 = pack_weight(wv[512:], "e2m1")
    return {
        "tab_words": p_tab[0],
        "tab_scales": p_tab[1],
        "wk_words": p_wk[0],
        "wk_scales": p_wk[1],
        "wv8": (wv[:512]).astype(np.float32),
        "wv4_words": p_wv4[0],
        "wv4_scales": p_wv4[1],
        "st": (n((N, J))).astype(np.float32),
        "res": (n((N, J))).astype(np.float32),
        "offs": striped(np.random.permutation(T)[:J]),
    }


def reference(tab_words, tab_scales, wk_words, wk_scales, wv8, wv4_words, wv4_scales, st, res, offs):
    idx = unstriped(offs)
    tab_ = unpack_weight(tab_words, tab_scales, "e4m3")[:, idx]
    wk_ = unpack_weight(wk_words, wk_scales, "e4m3")
    wv8_ = mxq(f64(wv8), 0, "e4m3")
    wv4_ = unpack_weight(wv4_words, wv4_scales, "e2m1")
    ke = wk_.T @ tab_
    ve = wv8_.T @ tab_[:512] + wv4_.T @ tab_[512:]
    gate = sigm(ke * f64(st))
    return f64(res) + gate * ve

@@ -1,0 +1,178 @@
+from contextlib import ExitStack
+
+import concourse.mybir as mybir
+
+K, N, T, J = 1024, 512, 4096, 1024
+FLOPS = 2 * 2 * K * N * J
+
+F32 = mybir.dt.float32
+BF16 = mybir.dt.bfloat16
+I32 = mybir.dt.int32
+U32 = mybir.dt.uint32
+U16 = mybir.dt.uint16
+U8 = mybir.dt.uint8
+FP8X4 = mybir.dt.float8_e4m3fn_x4
+FP4X4 = mybir.dt.float4_e2m1fn_x4
+MULT = mybir.AluOpType.mult
+ADD = mybir.AluOpType.add
+SIGMOID = mybir.ActivationFunctionType.Sigmoid
+
+P = 128
+PACK = 4
+HALF = 512
+CHUNKS = N // P
+HALVES = J // HALF
+SCALE_ROW0 = (4, 0)
+
+
+def tile_list_engram_qf_sig_kernel(
+    tc, tab_words, tab_scales, wk_words, wk_scales, wv8, wv4_words, wv4_scales, st, res, offs, out
+):
+    nc = tc.nc
+    with ExitStack() as ctx:
+        keep = ctx.enter_context(tc.tile_pool(name="keep", bufs=1))
+        work = ctx.enter_context(tc.tile_pool(name="work", bufs=3))
+        psum = ctx.enter_context(tc.psum_pool(name="psum", bufs=4))
+
+        offsets = keep.tile([P, J // 16], U16, name="offsets")
+        table = [keep.tile([P, T], U32, name="table%d" % a, align_bytes=64) for a in range(2)]
+        table_scales = keep.tile([P, T], U8, name="table_scales", align_bytes=64)
+        wk_planes = keep.tile([P, 2, N], U8, name="wk_planes", align_bytes=64)
+        wv4_plane = keep.tile([P, N], U8, name="wv4_plane", align_bytes=64)
+        wk_sb = [keep.tile([P, N], U32, name="wk%d" % a, align_bytes=64) for a in range(2)]
+        wv4_sb = keep.tile([P, 2 * N], U8, name="wv4_sb", align_bytes=64)
+        wv8_raw = keep.tile([P, PACK, N], F32, name="wv8_raw", align_bytes=64)
+        wv8_bf = keep.tile([P, N, PACK], BF16, name="wv8_bf", align_bytes=64)
+        wv8_codes = keep.tile([P, N], U32, name="wv8_codes", align_bytes=64)
+        wv8_scales = keep.tile([P, N], U8, name="wv8_scales", align_bytes=64)
+        st_sb = [keep.tile([P, J], F32, name="st%d" % c) for c in range(CHUNKS)]
+        res_sb = [keep.tile([P, J], F32, name="res%d" % c) for c in range(CHUNKS)]
+        out_sb = [keep.tile([P, J], F32, name="out%d" % c) for c in range(CHUNKS)]
+        gated = [keep.tile([P, J], F32, name="gated%d" % c) for c in range(CHUNKS)]
+        picked0 = keep.tile([P, J], U32, name="picked0", align_bytes=64)
+        picked1 = [keep.tile([P, HALF], U32, name="picked1_%d" % h, align_bytes=64) for h in range(HALVES)]
+        picked_scales = keep.tile([P, J], U8, name="picked_scales", align_bytes=64)
+        warm_in = keep.tile([P, 1], F32, name="warm_in")
+        warm_out = keep.tile([P, 1], F32, name="warm_out")
+
+        nc.vector.memset(wk_planes[:].bitcast(I32), 0)
+        nc.vector.memset(wv4_plane[:].bitcast(I32), 0)
+        nc.vector.memset(table_scales[:].bitcast(I32), 0)
+        nc.vector.memset(warm_in[:], 0.0)
+        nc.scalar.activation(warm_out[:], warm_in[:], SIGMOID)
+
+        def load_table(a, cols):
+            nc.sync.dma_start(
+                table[a][:, cols].bitcast(I32), tab_words[a, :, cols, :].rearrange("p t i -> p (t i)").bitcast(I32)
+            )
+
+        def load_wk(a):
+            nc.sync.dma_start(wk_sb[a][:].bitcast(I32), wk_words[a].rearrange("p n i -> p (n i)").bitcast(I32))
+
+        def load_wv4_scales(r):
+            nc.sync.dma_start(wv4_plane[r:P:32, :].bitcast(I32), wv4_scales[0, r:16:4, :].bitcast(I32))
+
+        for a in range(2):
+            for r in range(4):
+                nc.gpsimd.dma_start(
+                    table_scales[SCALE_ROW0[a] + r : P : 32, :].bitcast(I32), tab_scales[a, r:16:4, :].bitcast(I32)
+                )
+        nc.sync.dma_start(offsets[:], offs)
+        load_table(0, slice(0, T // 2))
+        load_table(0, slice(T // 2, T))
+        for r in range(4):
+            nc.sync.dma_start(
+                wk_planes[r:P:32, :, :].bitcast(I32),
+                wk_scales[:, r:16:4, :].rearrange("a q n -> q a n").bitcast(I32),
+            )
+        load_wv4_scales(0)
+        nc.sync.dma_start(wv8_raw[:], wv8.rearrange("(p i) n -> p i n", i=PACK))
+        load_wk(0)
+        load_table(1, slice(0, T))
+        for r in range(1, 4):
+            load_wv4_scales(r)
+        load_wk(1)
+        nc.sync.dma_start(wv4_sb[:].bitcast(I32), wv4_words[0].bitcast(I32))
+        for c in range(CHUNKS + 1):
+            if c < CHUNKS:
+                nc.sync.dma_start(st_sb[c][:], st[c * P : (c + 1) * P, :])
+            if c > 0:
+                nc.sync.dma_start(res_sb[c - 1][:], res[(c - 1) * P : c * P, :])
+
+        nc.vector.tensor_copy(picked0[:], table[0][:].indirect(offsets[:]))
+        nc.vector.tensor_copy(picked_scales[:], table_scales[:].indirect(offsets[:]))
+        nc.scalar.copy(wv8_bf[:], wv8_raw[:].rearrange("p i n -> p n i"))
+        nc.vector.quantize_mx(
+            out=wv8_codes[:].bitcast(FP8X4), scales=wv8_scales[:], in_=wv8_bf[:].rearrange("p n i -> p (n i)")
+        )
+        for h in range(HALVES):
+            nc.vector.tensor_copy(picked1[h][:], table[1][:].indirect(offsets[:, h * 32 : (h + 1) * 32]))
+
+        def picked(a, h):
+            cols = slice(h * HALF, (h + 1) * HALF)
+            words = picked0[:, cols] if a == 0 else picked1[h][:]
+            return dict(rhs=words.bitcast(FP8X4), rhs_scale=picked_scales[SCALE_ROW0[a] : P, cols])
+
+        def key(c, h):
+            rows = slice(c * P, (c + 1) * P)
+            ke = psum.tile([P, HALF], F32, name="ke")
+            for a in range(2):
+                nc.tensor.matmul_mx(
+                    out=ke[:],
+                    lhsT=wk_sb[a][:, rows].bitcast(FP8X4),
+                    lhsT_scale=wk_planes[:, a, rows],
+                    start=(a == 0),
+                    stop=(a == 1),
+                    **picked(a, h),
+                )
+            return ke
+
+        def value(c, h):
+            rows = slice(c * P, (c + 1) * P)
+            ve = psum.tile([P, HALF], F32, name="ve")
+            nc.tensor.matmul_mx(
+                out=ve[:],
+                lhsT=wv8_codes[:, rows].bitcast(FP8X4),
+                lhsT_scale=wv8_scales[:, rows],
+                start=True,
+                stop=False,
+                **picked(0, h),
+            )
+            nc.tensor.matmul_mx(
+                out=ve[:],
+                lhsT=wv4_sb[:, 2 * c * P : 2 * (c + 1) * P].bitcast(FP4X4),
+                lhsT_scale=wv4_plane[:, rows],
+                start=False,
+                stop=True,
+                **picked(1, h),
+            )
+            return ve
+
+        def gate(c, h, ke):
+            cols = slice(h * HALF, (h + 1) * HALF)
+            logit = work.tile([P, HALF], F32, name="logit")
+            nc.vector.tensor_tensor(logit[:], ke[:], st_sb[c][:, cols], MULT)
+            opened = work.tile([P, HALF], F32, name="opened")
+            nc.scalar.activation(opened[:], logit[:], SIGMOID)
+            return opened
+
+        def finish(c, h, opened):
+            rows = slice(c * P, (c + 1) * P)
+            cols = slice(h * HALF, (h + 1) * HALF)
+            ve = value(c, h)
+            nc.vector.tensor_tensor(gated[c][:, cols], ve[:], opened[:], MULT)
+            adder = nc.vector if c == CHUNKS - 1 else nc.gpsimd
+            adder.tensor_tensor(out_sb[c][:, cols], gated[c][:, cols], res_sb[c][:, cols], ADD)
+            if c == CHUNKS - 1:
+                nc.sync.dma_start(out[rows, cols], out_sb[c][:, cols])
+            elif h == HALVES - 1:
+                nc.sync.dma_start(out[rows, :], out_sb[c][:])
+
+        pending = None
+        for c in range(CHUNKS):
+            for h in range(HALVES):
+                opened = gate(c, h, key(c, h))
+                if pending is not None:
+                    finish(*pending)
+                pending = (c, h, opened)
+        finish(*pending)

@@ -41,23 +41,26 @@ def tile_list_engram_qf_sig_kernel(
         wv4_plane = keep.tile([P, N], U8, name="wv4_plane", align_bytes=64)
         wk_sb = [keep.tile([P, N], U32, name="wk%d" % a, align_bytes=64) for a in range(2)]
         wv4_sb = keep.tile([P, 2 * N], U8, name="wv4_sb", align_bytes=64)
-        wv8_raw = keep.tile([P, PACK, N], F32, name="wv8_raw", align_bytes=64)
-        wv8_bf = keep.tile([P, N, PACK], BF16, name="wv8_bf", align_bytes=64)
-        wv8_codes = keep.tile([P, N], U32, name="wv8_codes", align_bytes=64)
-        wv8_scales = keep.tile([P, N], U8, name="wv8_scales", align_bytes=64)
+        wv8_raw = [keep.tile([P, PACK, N // 2], F32, name="wv8_raw%d" % u, align_bytes=64) for u in range(2)]
+        wv8_bf = [keep.tile([P, N // 2, PACK], BF16, name="wv8_bf%d" % u, align_bytes=64) for u in range(2)]
+        wv8_codes = [keep.tile([P, N // 2], U32, name="wv8_codes%d" % u, align_bytes=64) for u in range(2)]
+        wv8_plane = [keep.tile([P, N // 2], U8, name="wv8_plane%d" % u, align_bytes=64) for u in range(2)]
         st_sb = [keep.tile([P, J], F32, name="st%d" % c) for c in range(CHUNKS)]
         res_sb = [keep.tile([P, J], F32, name="res%d" % c) for c in range(CHUNKS)]
         out_sb = [keep.tile([P, J], F32, name="out%d" % c) for c in range(CHUNKS)]
         gated = [keep.tile([P, J], F32, name="gated%d" % c) for c in range(CHUNKS)]
-        picked0 = keep.tile([P, J], U32, name="picked0", align_bytes=64)
-        picked1 = [keep.tile([P, HALF], U32, name="picked1_%d" % h, align_bytes=64) for h in range(HALVES)]
+        picked_words = [
+            [keep.tile([P, HALF], U32, name="picked%d_%d" % (a, h), align_bytes=64) for h in range(HALVES)]
+            for a in range(2)
+        ]
         picked_scales = keep.tile([P, J], U8, name="picked_scales", align_bytes=64)
+        picked_planes = keep.tile([P, J], U8, name="picked_planes", align_bytes=64)
         warm_in = keep.tile([P, 1], F32, name="warm_in")
         warm_out = keep.tile([P, 1], F32, name="warm_out")
 
+        nc.vector.memset(table_scales[:].bitcast(I32), 0)
         nc.vector.memset(wk_planes[:].bitcast(I32), 0)
         nc.vector.memset(wv4_plane[:].bitcast(I32), 0)
-        nc.vector.memset(table_scales[:].bitcast(I32), 0)
         nc.vector.memset(warm_in[:], 0.0)
         nc.scalar.activation(warm_out[:], warm_in[:], SIGMOID)
 
@@ -72,46 +75,76 @@ def tile_list_engram_qf_sig_kernel(
         def load_wv4_scales(r):
             nc.sync.dma_start(wv4_plane[r:P:32, :].bitcast(I32), wv4_scales[0, r:16:4, :].bitcast(I32))
 
-        for a in range(2):
-            for r in range(4):
-                nc.gpsimd.dma_start(
-                    table_scales[SCALE_ROW0[a] + r : P : 32, :].bitcast(I32), tab_scales[a, r:16:4, :].bitcast(I32)
-                )
-        nc.sync.dma_start(offsets[:], offs)
-        load_table(0, slice(0, T // 2))
-        load_table(0, slice(T // 2, T))
-        for r in range(4):
+        def load_table_scales(a):
+            nc.sync.dma_start(table_scales[3 * (1 - a) : 96 : 6, :].bitcast(I32), tab_scales[a].bitcast(I32))
+
+        def place_picked_scales(r):
+            nc.sync.dma_start(
+                picked_planes[r:P:4, :].bitcast(I32), picked_scales[6 * r : 6 * r + 94 : 3, :].bitcast(I32)
+            )
+
+        def load_wk_scales(r):
             nc.sync.dma_start(
                 wk_planes[r:P:32, :, :].bitcast(I32),
                 wk_scales[:, r:16:4, :].rearrange("a q n -> q a n").bitcast(I32),
             )
-        load_wv4_scales(0)
-        nc.sync.dma_start(wv8_raw[:], wv8.rearrange("(p i) n -> p i n", i=PACK))
-        load_wk(0)
-        load_table(1, slice(0, T))
-        for r in range(1, 4):
-            load_wv4_scales(r)
-        load_wk(1)
-        nc.sync.dma_start(wv4_sb[:].bitcast(I32), wv4_words[0].bitcast(I32))
-        for c in range(CHUNKS + 1):
-            if c < CHUNKS:
-                nc.sync.dma_start(st_sb[c][:], st[c * P : (c + 1) * P, :])
-            if c > 0:
-                nc.sync.dma_start(res_sb[c - 1][:], res[(c - 1) * P : c * P, :])
 
-        nc.vector.tensor_copy(picked0[:], table[0][:].indirect(offsets[:]))
+        def load_wv8(u):
+            cols = slice(u * N // 2, (u + 1) * N // 2)
+            nc.sync.dma_start(wv8_raw[u][:], wv8[:, cols].rearrange("(p i) n -> p i n", i=PACK))
+
+        def load_rows(tiles, source, c):
+            nc.sync.dma_start(tiles[c][:], source[c * P : (c + 1) * P, :])
+
+        halves = (slice(0, T // 2), slice(T // 2, T))
+        nc.sync.dma_start(offsets[:], offs)
+        load_table(0, halves[0])
+        load_table_scales(0)
+        load_table_scales(1)
+        load_table(0, halves[1])
+        load_wk(0)
+        for r in range(4):
+            load_wk_scales(r)
+        load_wv8(0)
+        load_table(1, halves[0])
         nc.vector.tensor_copy(picked_scales[:], table_scales[:].indirect(offsets[:]))
-        nc.scalar.copy(wv8_bf[:], wv8_raw[:].rearrange("p i n -> p n i"))
-        nc.vector.quantize_mx(
-            out=wv8_codes[:].bitcast(FP8X4), scales=wv8_scales[:], in_=wv8_bf[:].rearrange("p n i -> p (n i)")
-        )
+        for r in range(4):
+            place_picked_scales(r)
+        load_table(1, halves[1])
+        load_wv4_scales(0)
+        load_wv4_scales(1)
+        load_wk(1)
+        load_wv4_scales(2)
+        load_wv4_scales(3)
+        load_wv8(1)
+        load_rows(st_sb, st, 0)
+        nc.sync.dma_start(wv4_sb[:].bitcast(I32), wv4_words[0].bitcast(I32))
+        load_rows(st_sb, st, 1)
+        for c in range(CHUNKS):
+            load_rows(res_sb, res, c)
+            if c + 2 < CHUNKS:
+                load_rows(st_sb, st, c + 2)
+
+        def quantise_wv8(u):
+            nc.scalar.copy(wv8_bf[u][:], wv8_raw[u][:].rearrange("p i n -> p n i"))
+            nc.vector.quantize_mx(
+                out=wv8_codes[u][:].bitcast(FP8X4),
+                scales=wv8_plane[u][:],
+                in_=wv8_bf[u][:].rearrange("p n i -> p (n i)"),
+            )
+
+        def gather(dst, window, h):
+            nc.vector.tensor_copy(dst[:], window[:].indirect(offsets[:, h * HALF // 16 : (h + 1) * HALF // 16]))
+
         for h in range(HALVES):
-            nc.vector.tensor_copy(picked1[h][:], table[1][:].indirect(offsets[:, h * 32 : (h + 1) * 32]))
+            gather(picked_words[0][h], table[0], h)
+        quantise_wv8(0)
+        for h in range(HALVES):
+            gather(picked_words[1][h], table[1], h)
+        quantise_wv8(1)
 
         def picked(a, h):
-            cols = slice(h * HALF, (h + 1) * HALF)
-            words = picked0[:, cols] if a == 0 else picked1[h][:]
-            return dict(rhs=words.bitcast(FP8X4), rhs_scale=picked_scales[SCALE_ROW0[a] : P, cols])
+            return dict(rhs=picked_words[a][h][:].bitcast(FP8X4), rhs_scale=picked_planes[SCALE_ROW0[a] : P, h * HALF : (h + 1) * HALF])
 
         def key(c, h):
             rows = slice(c * P, (c + 1) * P)
@@ -129,11 +162,12 @@ def tile_list_engram_qf_sig_kernel(
 
         def value(c, h):
             rows = slice(c * P, (c + 1) * P)
+            within = slice(c % 2 * P, (c % 2 + 1) * P)
             ve = psum.tile([P, HALF], F32, name="ve")
             nc.tensor.matmul_mx(
                 out=ve[:],
-                lhsT=wv8_codes[:, rows].bitcast(FP8X4),
-                lhsT_scale=wv8_scales[:, rows],
+                lhsT=wv8_codes[c // 2][:, within].bitcast(FP8X4),
+                lhsT_scale=wv8_plane[c // 2][:, within],
                 start=True,
                 stop=False,
                 **picked(0, h),
@@ -163,7 +197,7 @@ def tile_list_engram_qf_sig_kernel(
             nc.vector.tensor_tensor(gated[c][:, cols], ve[:], opened[:], MULT)
             adder = nc.vector if c == CHUNKS - 1 else nc.gpsimd
             adder.tensor_tensor(out_sb[c][:, cols], gated[c][:, cols], res_sb[c][:, cols], ADD)
-            if c == CHUNKS - 1:
+            if c >= CHUNKS // 2:
                 nc.sync.dma_start(out[rows, cols], out_sb[c][:, cols])
             elif h == HALVES - 1:
                 nc.sync.dma_start(out[rows, :], out_sb[c][:])

@@ -97,8 +97,8 @@ def tile_list_engram_qf_sig_kernel(
             nc.sync.dma_start(tiles[c][:], source[c * P : (c + 1) * P, :])
 
         halves = (slice(0, T // 2), slice(T // 2, T))
-        nc.sync.dma_start(offsets[:], offs)
         load_table(0, halves[0])
+        nc.sync.dma_start(offsets[:], offs)
         load_table_scales(0)
         load_table_scales(1)
         load_table(0, halves[1])
@@ -117,8 +117,9 @@ def tile_list_engram_qf_sig_kernel(
         load_wv4_scales(2)
         load_wv4_scales(3)
         load_wv8(1)
-        load_rows(st_sb, st, 0)
+        nc.sync.dma_start(st_sb[0][:, :HALF], st[:P, :HALF])
         nc.sync.dma_start(wv4_sb[:].bitcast(I32), wv4_words[0].bitcast(I32))
+        nc.sync.dma_start(st_sb[0][:, HALF:], st[:P, HALF:])
         load_rows(st_sb, st, 1)
         for c in range(CHUNKS):
             load_rows(res_sb, res, c)
@@ -196,6 +197,12 @@ def tile_list_engram_qf_sig_kernel(
             ve = value(c, h)
             nc.vector.tensor_tensor(gated[c][:, cols], ve[:], opened[:], MULT)
             adder = nc.vector if c == CHUNKS - 1 else nc.gpsimd
+            if (c, h) == (CHUNKS - 1, HALVES - 1):
+                for first in range(h * HALF, J, HALF // 2):
+                    part = slice(first, first + HALF // 2)
+                    adder.tensor_tensor(out_sb[c][:, part], gated[c][:, part], res_sb[c][:, part], ADD)
+                    nc.sync.dma_start(out[rows, part], out_sb[c][:, part])
+                return
             adder.tensor_tensor(out_sb[c][:, cols], gated[c][:, cols], res_sb[c][:, cols], ADD)
             if c >= CHUNKS // 2:
                 nc.sync.dma_start(out[rows, cols], out_sb[c][:, cols])

@@ -20,6 +20,7 @@ SIGMOID = mybir.ActivationFunctionType.Sigmoid
 P = 128
 PACK = 4
 HALF = 512
+QUARTER = 256
 CHUNKS = N // P
 HALVES = J // HALF
 SCALE_ROW0 = (4, 0)
@@ -196,14 +197,9 @@ def tile_list_engram_qf_sig_kernel(
             cols = slice(h * HALF, (h + 1) * HALF)
             ve = value(c, h)
             nc.vector.tensor_tensor(gated[c][:, cols], ve[:], opened[:], MULT)
-            adder = nc.vector if c == CHUNKS - 1 else nc.gpsimd
-            if (c, h) == (CHUNKS - 1, HALVES - 1):
-                for first in range(h * HALF, J, HALF // 2):
-                    part = slice(first, first + HALF // 2)
-                    adder.tensor_tensor(out_sb[c][:, part], gated[c][:, part], res_sb[c][:, part], ADD)
-                    nc.sync.dma_start(out[rows, part], out_sb[c][:, part])
-                return
-            adder.tensor_tensor(out_sb[c][:, cols], gated[c][:, cols], res_sb[c][:, cols], ADD)
+            if c == CHUNKS - 1:
+                cols = slice(0, QUARTER)
+            nc.gpsimd.tensor_tensor(out_sb[c][:, cols], gated[c][:, cols], res_sb[c][:, cols], ADD)
             if c >= CHUNKS // 2:
                 nc.sync.dma_start(out[rows, cols], out_sb[c][:, cols])
             elif h == HALVES - 1:
@@ -212,8 +208,30 @@ def tile_list_engram_qf_sig_kernel(
         pending = None
         for c in range(CHUNKS):
             for h in range(HALVES):
+                if (c, h) == (CHUNKS - 1, HALVES - 1):
+                    break
                 opened = gate(c, h, key(c, h))
                 if pending is not None:
                     finish(*pending)
                 pending = (c, h, opened)
+
+        c, h = CHUNKS - 1, HALVES - 1
+        ke = key(c, h)
+        logit = work.tile([P, HALF], F32, name="logit")
+        last_opened = work.tile([P, HALF], F32, name="opened")
+        gates = (out_sb[c][:, QUARTER:HALF], last_opened[:, QUARTER:])
+        for q in range(2):
+            part = slice(q * QUARTER, (q + 1) * QUARTER)
+            cols = slice(HALF + q * QUARTER, HALF + (q + 1) * QUARTER)
+            nc.vector.tensor_tensor(logit[:, part], ke[:, part], st_sb[c][:, cols], MULT)
+            nc.scalar.activation(gates[q], logit[:, part], SIGMOID)
         finish(*pending)
+        ve = value(c, h)
+        for q in range(2):
+            part = slice(q * QUARTER, (q + 1) * QUARTER)
+            cols = slice(HALF + q * QUARTER, HALF + (q + 1) * QUARTER)
+            nc.vector.tensor_tensor(gated[c][:, cols], ve[:, part], gates[q], MULT)
+        for first in range(QUARTER, J, QUARTER):
+            cols = slice(first, first + QUARTER)
+            nc.vector.tensor_tensor(out_sb[c][:, cols], gated[c][:, cols], res_sb[c][:, cols], ADD)
+            nc.scalar.dma_start(out[c * P :, cols], out_sb[c][:, cols])

@@ -21,6 +21,7 @@ P = 128
 PACK = 4
 HALF = 512
 QUARTER = 256
+GPSIMD_ADDS = 5
 CHUNKS = N // P
 HALVES = J // HALF
 SCALE_ROW0 = (4, 0)
@@ -197,8 +198,8 @@ def tile_list_engram_qf_sig_kernel(
             cols = slice(h * HALF, (h + 1) * HALF)
             ve = value(c, h)
             nc.vector.tensor_tensor(gated[c][:, cols], ve[:], opened[:], MULT)
-            if c == CHUNKS - 1:
-                cols = slice(0, QUARTER)
+            if c * HALVES + h >= GPSIMD_ADDS:
+                return
             nc.gpsimd.tensor_tensor(out_sb[c][:, cols], gated[c][:, cols], res_sb[c][:, cols], ADD)
             if c >= CHUNKS // 2:
                 nc.sync.dma_start(out[rows, cols], out_sb[c][:, cols])
@@ -218,8 +219,7 @@ def tile_list_engram_qf_sig_kernel(
         c, h = CHUNKS - 1, HALVES - 1
         ke = key(c, h)
         logit = work.tile([P, HALF], F32, name="logit")
-        last_opened = work.tile([P, HALF], F32, name="opened")
-        gates = (out_sb[c][:, QUARTER:HALF], last_opened[:, QUARTER:])
+        gates = (out_sb[c - 1][:, HALF : HALF + QUARTER], out_sb[c][:, :QUARTER])
         for q in range(2):
             part = slice(q * QUARTER, (q + 1) * QUARTER)
             cols = slice(HALF + q * QUARTER, HALF + (q + 1) * QUARTER)
@@ -231,7 +231,7 @@ def tile_list_engram_qf_sig_kernel(
             part = slice(q * QUARTER, (q + 1) * QUARTER)
             cols = slice(HALF + q * QUARTER, HALF + (q + 1) * QUARTER)
             nc.vector.tensor_tensor(gated[c][:, cols], ve[:, part], gates[q], MULT)
-        for first in range(QUARTER, J, QUARTER):
-            cols = slice(first, first + QUARTER)
+        for c, first, width in ((c - 1, HALF, HALF), (c, 0, HALF), (c, HALF, QUARTER), (c, HALF + QUARTER, QUARTER)):
+            cols = slice(first, first + width)
             nc.vector.tensor_tensor(out_sb[c][:, cols], gated[c][:, cols], res_sb[c][:, cols], ADD)
-            nc.scalar.dma_start(out[c * P :, cols], out_sb[c][:, cols])
+            nc.sync.dma_start(out[c * P : (c + 1) * P, cols], out_sb[c][:, cols])

@@ -33,7 +33,7 @@ def tile_list_engram_qf_sig_kernel(
     nc = tc.nc
     with ExitStack() as ctx:
         keep = ctx.enter_context(tc.tile_pool(name="keep", bufs=1))
-        work = ctx.enter_context(tc.tile_pool(name="work", bufs=3))
+        work = ctx.enter_context(tc.tile_pool(name="work", bufs=4))
         psum = ctx.enter_context(tc.psum_pool(name="psum", bufs=4))
 
         offsets = keep.tile([P, J // 16], U16, name="offsets")
@@ -78,11 +78,11 @@ def tile_list_engram_qf_sig_kernel(
             nc.sync.dma_start(wv4_plane[r:P:32, :].bitcast(I32), wv4_scales[0, r:16:4, :].bitcast(I32))
 
         def load_table_scales(a):
-            nc.sync.dma_start(table_scales[3 * (1 - a) : 96 : 6, :].bitcast(I32), tab_scales[a].bitcast(I32))
+            nc.sync.dma_start(table_scales[32 + 2 * (1 - a) : 96 : 4, :].bitcast(I32), tab_scales[a].bitcast(I32))
 
         def place_picked_scales(r):
             nc.sync.dma_start(
-                picked_planes[r:P:4, :].bitcast(I32), picked_scales[6 * r : 6 * r + 94 : 3, :].bitcast(I32)
+                picked_planes[r:P:4, :].bitcast(I32), picked_scales[32 + 4 * r : 95 + 4 * r : 2, :].bitcast(I32)
             )
 
         def load_wk_scales(r):
@@ -113,20 +113,20 @@ def tile_list_engram_qf_sig_kernel(
         for r in range(4):
             place_picked_scales(r)
         load_table(1, halves[1])
-        load_wv4_scales(0)
-        load_wv4_scales(1)
-        load_wk(1)
-        load_wv4_scales(2)
-        load_wv4_scales(3)
+        for r in range(4):
+            load_wv4_scales(r)
         load_wv8(1)
+        load_wk(1)
         nc.sync.dma_start(st_sb[0][:, :HALF], st[:P, :HALF])
         nc.sync.dma_start(wv4_sb[:].bitcast(I32), wv4_words[0].bitcast(I32))
         nc.sync.dma_start(st_sb[0][:, HALF:], st[:P, HALF:])
-        load_rows(st_sb, st, 1)
-        for c in range(CHUNKS):
+        for cols in (slice(0, HALF), slice(HALF, J)):
+            nc.sync.dma_start(st_sb[1][:, cols], st[P : 2 * P, cols])
+            nc.sync.dma_start(res_sb[0][:, cols], res[:P, cols])
+        for c in range(1, CHUNKS):
+            if c + 1 < CHUNKS:
+                load_rows(st_sb, st, c + 1)
             load_rows(res_sb, res, c)
-            if c + 2 < CHUNKS:
-                load_rows(st_sb, st, c + 2)
 
         def quantise_wv8(u):
             nc.scalar.copy(wv8_bf[u][:], wv8_raw[u][:].rearrange("p i n -> p n i"))
@@ -185,53 +185,58 @@ def tile_list_engram_qf_sig_kernel(
             )
             return ve
 
-        def gate(c, h, ke):
-            cols = slice(h * HALF, (h + 1) * HALF)
+        def columns(h):
+            return slice(h * HALF, (h + 1) * HALF)
+
+        def gated_tile(c, h):
+            if h == 1 and 0 < c < CHUNKS - 1:
+                return st_sb[c + 1][:, :HALF]
+            return gated[c][:, columns(h)]
+
+        gates = {}
+
+        def gate(c, h):
+            ke = key(c, h)
             logit = work.tile([P, HALF], F32, name="logit")
-            nc.vector.tensor_tensor(logit[:], ke[:], st_sb[c][:, cols], MULT)
-            opened = work.tile([P, HALF], F32, name="opened")
-            nc.scalar.activation(opened[:], logit[:], SIGMOID)
-            return opened
+            nc.vector.tensor_tensor(logit[:], ke[:], st_sb[c][:, columns(h)], MULT)
+            if c == CHUNKS - 1:
+                opened = out_sb[c - 1 + h][:, columns(1 - h)]
+            else:
+                opened = work.tile([P, HALF], F32, name="opened")[:]
+            nc.scalar.activation(opened, logit[:], SIGMOID)
+            gates.update({(c, h): opened})
 
-        def finish(c, h, opened):
-            rows = slice(c * P, (c + 1) * P)
-            cols = slice(h * HALF, (h + 1) * HALF)
-            ve = value(c, h)
-            nc.vector.tensor_tensor(gated[c][:, cols], ve[:], opened[:], MULT)
-            if c * HALVES + h >= GPSIMD_ADDS:
-                return
-            nc.gpsimd.tensor_tensor(out_sb[c][:, cols], gated[c][:, cols], res_sb[c][:, cols], ADD)
-            if c >= CHUNKS // 2:
-                nc.sync.dma_start(out[rows, cols], out_sb[c][:, cols])
-            elif h == HALVES - 1:
-                nc.sync.dma_start(out[rows, :], out_sb[c][:])
+        def product(c, h):
+            nc.vector.tensor_tensor(gated_tile(c, h), value(c, h)[:], gates[(c, h)], MULT)
 
-        pending = None
-        for c in range(CHUNKS):
-            for h in range(HALVES):
-                if (c, h) == (CHUNKS - 1, HALVES - 1):
-                    break
-                opened = gate(c, h, key(c, h))
-                if pending is not None:
-                    finish(*pending)
-                pending = (c, h, opened)
+        def add(engine, c, h, part):
+            engine.tensor_tensor(
+                out_sb[c][:, columns(h)][:, part], gated_tile(c, h)[:, part], res_sb[c][:, columns(h)][:, part], ADD
+            )
 
-        c, h = CHUNKS - 1, HALVES - 1
-        ke = key(c, h)
-        logit = work.tile([P, HALF], F32, name="logit")
-        gates = (out_sb[c - 1][:, HALF : HALF + QUARTER], out_sb[c][:, :QUARTER])
-        for q in range(2):
-            part = slice(q * QUARTER, (q + 1) * QUARTER)
-            cols = slice(HALF + q * QUARTER, HALF + (q + 1) * QUARTER)
-            nc.vector.tensor_tensor(logit[:, part], ke[:, part], st_sb[c][:, cols], MULT)
-            nc.scalar.activation(gates[q], logit[:, part], SIGMOID)
-        finish(*pending)
-        ve = value(c, h)
-        for q in range(2):
-            part = slice(q * QUARTER, (q + 1) * QUARTER)
-            cols = slice(HALF + q * QUARTER, HALF + (q + 1) * QUARTER)
-            nc.vector.tensor_tensor(gated[c][:, cols], ve[:, part], gates[q], MULT)
-        for c, first, width in ((c - 1, HALF, HALF), (c, 0, HALF), (c, HALF, QUARTER), (c, HALF + QUARTER, QUARTER)):
-            cols = slice(first, first + width)
-            nc.vector.tensor_tensor(out_sb[c][:, cols], gated[c][:, cols], res_sb[c][:, cols], ADD)
+        def store(c, cols):
             nc.sync.dma_start(out[c * P : (c + 1) * P, cols], out_sb[c][:, cols])
+
+        gate(0, 0)
+        gate(0, 1)
+        product(0, 0)
+        gate(1, 0)
+        product(0, 1)
+        gate(1, 1)
+        product(1, 0)
+        for c in range(2, CHUNKS):
+            gate(c, 0)
+            gate(c, 1)
+            product(c - 1, 1)
+            product(c, 0)
+        product(CHUNKS - 1, 1)
+        for t in range(CHUNKS * HALVES):
+            c, h = divmod(t, HALVES)
+            if t < GPSIMD_ADDS:
+                add(nc.gpsimd, c, h, slice(0, HALF))
+                if h == 1 or t == GPSIMD_ADDS - 1:
+                    store(c, slice(0, (h + 1) * HALF))
+            else:
+                for q in range(2):
+                    add(nc.vector, c, h, slice(q * QUARTER, (q + 1) * QUARTER))
+                    store(c, slice(h * HALF + q * QUARTER, h * HALF + (q + 1) * QUARTER))

@@ -21,6 +21,7 @@ P = 128
 PACK = 4
 HALF = 512
 QUARTER = 256
+GPSIMD_EXTRA = 192
 GPSIMD_ADDS = 5
 CHUNKS = N // P
 HALVES = J // HALF
@@ -49,7 +50,8 @@ def tile_list_engram_qf_sig_kernel(
         wv8_plane = [keep.tile([P, N // 2], U8, name="wv8_plane%d" % u, align_bytes=64) for u in range(2)]
         st_sb = [keep.tile([P, J], F32, name="st%d" % c) for c in range(CHUNKS)]
         res_sb = [keep.tile([P, J], F32, name="res%d" % c) for c in range(CHUNKS)]
-        out_sb = [keep.tile([P, J], F32, name="out%d" % c) for c in range(CHUNKS)]
+        out_all = keep.tile([P, CHUNKS * J], F32, name="out_all")
+        out_sb = [out_all[:, c * J : (c + 1) * J] for c in range(CHUNKS)]
         gated = [keep.tile([P, J], F32, name="gated%d" % c) for c in range(CHUNKS)]
         picked_words = [
             [keep.tile([P, HALF], U32, name="picked%d_%d" % (a, h), align_bytes=64) for h in range(HALVES)]
@@ -195,12 +197,15 @@ def tile_list_engram_qf_sig_kernel(
 
         gates = {}
 
+        keys = {(c, h): key(c, h) for h in range(HALVES) for c in range(2)}
+
         def gate(c, h):
-            ke = key(c, h)
+            ke = keys[(c, h)] if (c, h) in keys else key(c, h)
             logit = work.tile([P, HALF], F32, name="logit")
             nc.vector.tensor_tensor(logit[:], ke[:], st_sb[c][:, columns(h)], MULT)
             if c == CHUNKS - 1:
-                opened = out_sb[c - 1 + h][:, columns(1 - h)]
+                first = GPSIMD_ADDS * HALF + GPSIMD_EXTRA + h * HALF
+                opened = out_all[:, first : first + HALF]
             else:
                 opened = work.tile([P, HALF], F32, name="opened")[:]
             nc.scalar.activation(opened, logit[:], SIGMOID)
@@ -236,7 +241,12 @@ def tile_list_engram_qf_sig_kernel(
                 add(nc.gpsimd, c, h, slice(0, HALF))
                 if h == 1 or t == GPSIMD_ADDS - 1:
                     store(c, slice(0, (h + 1) * HALF))
+            elif t == GPSIMD_ADDS:
+                for engine, part in ((nc.gpsimd, slice(0, GPSIMD_EXTRA)), (nc.vector, slice(GPSIMD_EXTRA, HALF))):
+                    add(engine, c, h, part)
+                    store(c, slice(h * HALF + part.start, h * HALF + part.stop))
             else:
-                for q in range(2):
-                    add(nc.vector, c, h, slice(q * QUARTER, (q + 1) * QUARTER))
-                    store(c, slice(h * HALF + q * QUARTER, h * HALF + (q + 1) * QUARTER))
+                edges = (0, QUARTER, HALF) if h == 0 else (0, QUARTER, QUARTER + P, HALF)
+                for first, end in zip(edges, edges[1:]):
+                    add(nc.vector, c, h, slice(first, end))
+                    store(c, slice(h * HALF + first, h * HALF + end))

@@ -20,8 +20,6 @@ SIGMOID = mybir.ActivationFunctionType.Sigmoid
 P = 128
 PACK = 4
 HALF = 512
-QUARTER = 256
-GPSIMD_EXTRA = 192
 GPSIMD_ADDS = 5
 CHUNKS = N // P
 HALVES = J // HALF
@@ -122,10 +120,7 @@ def tile_list_engram_qf_sig_kernel(
         nc.sync.dma_start(st_sb[0][:, :HALF], st[:P, :HALF])
         nc.sync.dma_start(wv4_sb[:].bitcast(I32), wv4_words[0].bitcast(I32))
         nc.sync.dma_start(st_sb[0][:, HALF:], st[:P, HALF:])
-        for cols in (slice(0, HALF), slice(HALF, J)):
-            nc.sync.dma_start(st_sb[1][:, cols], st[P : 2 * P, cols])
-            nc.sync.dma_start(res_sb[0][:, cols], res[:P, cols])
-        for c in range(1, CHUNKS):
+        for c in range(CHUNKS):
             if c + 1 < CHUNKS:
                 load_rows(st_sb, st, c + 1)
             load_rows(res_sb, res, c)
@@ -191,7 +186,7 @@ def tile_list_engram_qf_sig_kernel(
             return slice(h * HALF, (h + 1) * HALF)
 
         def gated_tile(c, h):
-            if h == 1 and 0 < c < CHUNKS - 1:
+            if h == 1 and c < CHUNKS - 1:
                 return st_sb[c + 1][:, :HALF]
             return gated[c][:, columns(h)]
 
@@ -204,7 +199,7 @@ def tile_list_engram_qf_sig_kernel(
             logit = work.tile([P, HALF], F32, name="logit")
             nc.vector.tensor_tensor(logit[:], ke[:], st_sb[c][:, columns(h)], MULT)
             if c == CHUNKS - 1:
-                first = GPSIMD_ADDS * HALF + GPSIMD_EXTRA + h * HALF
+                first = (GPSIMD_ADDS + h) * HALF
                 opened = out_all[:, first : first + HALF]
             else:
                 opened = work.tile([P, HALF], F32, name="opened")[:]
@@ -214,39 +209,23 @@ def tile_list_engram_qf_sig_kernel(
         def product(c, h):
             nc.vector.tensor_tensor(gated_tile(c, h), value(c, h)[:], gates[(c, h)], MULT)
 
-        def add(engine, c, h, part):
-            engine.tensor_tensor(
-                out_sb[c][:, columns(h)][:, part], gated_tile(c, h)[:, part], res_sb[c][:, columns(h)][:, part], ADD
-            )
+        def add(engine, c, h):
+            engine.tensor_tensor(out_sb[c][:, columns(h)], gated_tile(c, h), res_sb[c][:, columns(h)], ADD)
 
         def store(c, cols):
             nc.sync.dma_start(out[c * P : (c + 1) * P, cols], out_sb[c][:, cols])
 
-        gate(0, 0)
-        gate(0, 1)
-        product(0, 0)
-        gate(1, 0)
-        product(0, 1)
-        gate(1, 1)
-        product(1, 0)
-        for c in range(2, CHUNKS):
+        for c in range(CHUNKS):
             gate(c, 0)
             gate(c, 1)
-            product(c - 1, 1)
+            if c > 0:
+                product(c - 1, 1)
             product(c, 0)
         product(CHUNKS - 1, 1)
         for t in range(CHUNKS * HALVES):
             c, h = divmod(t, HALVES)
-            if t < GPSIMD_ADDS:
-                add(nc.gpsimd, c, h, slice(0, HALF))
-                if h == 1 or t == GPSIMD_ADDS - 1:
-                    store(c, slice(0, (h + 1) * HALF))
-            elif t == GPSIMD_ADDS:
-                for engine, part in ((nc.gpsimd, slice(0, GPSIMD_EXTRA)), (nc.vector, slice(GPSIMD_EXTRA, HALF))):
-                    add(engine, c, h, part)
-                    store(c, slice(h * HALF + part.start, h * HALF + part.stop))
-            else:
-                edges = (0, QUARTER, HALF) if h == 0 else (0, QUARTER, QUARTER + P, HALF)
-                for first, end in zip(edges, edges[1:]):
-                    add(nc.vector, c, h, slice(first, end))
-                    store(c, slice(h * HALF + first, h * HALF + end))
+            add(nc.gpsimd if t < GPSIMD_ADDS else nc.vector, c, h)
+            if c >= CHUNKS // 2:
+                store(c, columns(h))
+            elif h == 1:
+                store(c, slice(0, J))

@@ -21,6 +21,7 @@ P = 128
 PACK = 4
 HALF = 512
 GPSIMD_ADDS = 5
+VALUE_BANKS = {(2, 0): 4, (2, 1): 0, (3, 0): 1, (3, 1): 7}
 CHUNKS = N // P
 HALVES = J // HALF
 SCALE_ROW0 = (4, 0)
@@ -33,14 +34,15 @@ def tile_list_engram_qf_sig_kernel(
     with ExitStack() as ctx:
         keep = ctx.enter_context(tc.tile_pool(name="keep", bufs=1))
         work = ctx.enter_context(tc.tile_pool(name="work", bufs=4))
-        psum = ctx.enter_context(tc.psum_pool(name="psum", bufs=4))
+        psum = ctx.enter_context(tc.psum_pool(name="psum", bufs=1))
 
         offsets = keep.tile([P, J // 16], U16, name="offsets")
         table = [keep.tile([P, T], U32, name="table%d" % a, align_bytes=64) for a in range(2)]
         table_scales = keep.tile([P, T], U8, name="table_scales", align_bytes=64)
         wk_planes = keep.tile([P, 2, N], U8, name="wk_planes", align_bytes=64)
         wv4_plane = keep.tile([P, N], U8, name="wv4_plane", align_bytes=64)
-        wk_sb = [keep.tile([P, N], U32, name="wk%d" % a, align_bytes=64) for a in range(2)]
+        wk_early = [keep.tile([P, N // 2], U32, name="wk_early%d" % a, align_bytes=64) for a in range(2)]
+        wk_late = keep.tile([P, 2, N // 2], U32, name="wk_late", align_bytes=64)
         wv4_sb = keep.tile([P, 2 * N], U8, name="wv4_sb", align_bytes=64)
         wv8_raw = [keep.tile([P, PACK, N // 2], F32, name="wv8_raw%d" % u, align_bytes=64) for u in range(2)]
         wv8_bf = [keep.tile([P, N // 2, PACK], BF16, name="wv8_bf%d" % u, align_bytes=64) for u in range(2)]
@@ -71,8 +73,15 @@ def tile_list_engram_qf_sig_kernel(
                 table[a][:, cols].bitcast(I32), tab_words[a, :, cols, :].rearrange("p t i -> p (t i)").bitcast(I32)
             )
 
-        def load_wk(a):
-            nc.sync.dma_start(wk_sb[a][:].bitcast(I32), wk_words[a].rearrange("p n i -> p (n i)").bitcast(I32))
+        def load_wk_early(a):
+            nc.sync.dma_start(
+                wk_early[a][:].bitcast(I32), wk_words[a, :, : N // 2, :].rearrange("p n i -> p (n i)").bitcast(I32)
+            )
+
+        def load_wk_late():
+            nc.sync.dma_start(
+                wk_late[:].bitcast(I32), wk_words[:, :, N // 2 :, :].rearrange("a p n i -> p a (n i)").bitcast(I32)
+            )
 
         def load_wv4_scales(r):
             nc.sync.dma_start(wv4_plane[r:P:32, :].bitcast(I32), wv4_scales[0, r:16:4, :].bitcast(I32))
@@ -104,7 +113,7 @@ def tile_list_engram_qf_sig_kernel(
         load_table_scales(0)
         load_table_scales(1)
         load_table(0, halves[1])
-        load_wk(0)
+        load_wk_early(0)
         for r in range(4):
             load_wk_scales(r)
         load_wv8(0)
@@ -116,7 +125,7 @@ def tile_list_engram_qf_sig_kernel(
         for r in range(4):
             load_wv4_scales(r)
         load_wv8(1)
-        load_wk(1)
+        load_wk_early(1)
         nc.sync.dma_start(st_sb[0][:, :HALF], st[:P, :HALF])
         nc.sync.dma_start(wv4_sb[:].bitcast(I32), wv4_words[0].bitcast(I32))
         nc.sync.dma_start(st_sb[0][:, HALF:], st[:P, HALF:])
@@ -124,6 +133,8 @@ def tile_list_engram_qf_sig_kernel(
             if c + 1 < CHUNKS:
                 load_rows(st_sb, st, c + 1)
             load_rows(res_sb, res, c)
+            if c == 0:
+                load_wk_late()
 
         def quantise_wv8(u):
             nc.scalar.copy(wv8_bf[u][:], wv8_raw[u][:].rearrange("p i n -> p n i"))
@@ -148,11 +159,13 @@ def tile_list_engram_qf_sig_kernel(
 
         def key(c, h):
             rows = slice(c * P, (c + 1) * P)
-            ke = psum.tile([P, HALF], F32, name="ke")
+            ke = psum.tile([P, HALF], F32, name="bank%d" % (2 * (c % 2) + h))
+            within = slice(c % 2 * P, (c % 2 + 1) * P)
             for a in range(2):
+                words = wk_early[a][:, within] if c < 2 else wk_late[:, a, within]
                 nc.tensor.matmul_mx(
                     out=ke[:],
-                    lhsT=wk_sb[a][:, rows].bitcast(FP8X4),
+                    lhsT=words.bitcast(FP8X4),
                     lhsT_scale=wk_planes[:, a, rows],
                     start=(a == 0),
                     stop=(a == 1),
@@ -163,7 +176,8 @@ def tile_list_engram_qf_sig_kernel(
         def value(c, h):
             rows = slice(c * P, (c + 1) * P)
             within = slice(c % 2 * P, (c % 2 + 1) * P)
-            ve = psum.tile([P, HALF], F32, name="ve")
+            b = 4 + 2 * c + h if c < 2 else VALUE_BANKS[(c, h)]
+            ve = psum.tile([P, HALF], F32, name="bank%d" % b)
             nc.tensor.matmul_mx(
                 out=ve[:],
                 lhsT=wv8_codes[c // 2][:, within].bitcast(FP8X4),

@@ -40,7 +40,6 @@ def tile_list_engram_qf_sig_kernel(
         table = [keep.tile([P, T], U32, name="table%d" % a, align_bytes=64) for a in range(2)]
         table_scales = keep.tile([P, T], U8, name="table_scales", align_bytes=64)
         wk_planes = keep.tile([P, 2, N], U8, name="wk_planes", align_bytes=64)
-        wv4_plane = keep.tile([P, N], U8, name="wv4_plane", align_bytes=64)
         wk_early = [keep.tile([P, N // 2], U32, name="wk_early%d" % a, align_bytes=64) for a in range(2)]
         wk_late = keep.tile([P, 2, N // 2], U32, name="wk_late", align_bytes=64)
         wv4_sb = keep.tile([P, 2 * N], U8, name="wv4_sb", align_bytes=64)
@@ -58,13 +57,15 @@ def tile_list_engram_qf_sig_kernel(
             for a in range(2)
         ]
         picked_scales = keep.tile([P, J], U8, name="picked_scales", align_bytes=64)
-        picked_planes = keep.tile([P, J], U8, name="picked_planes", align_bytes=64)
+        staged = keep.tile([P, J + N], U8, name="staged", align_bytes=64)
+        picked_planes = keep.tile([P, J + N], U8, name="picked_planes", align_bytes=64)
+        wv4_plane = picked_planes[:, J:]
         warm_in = keep.tile([P, 1], F32, name="warm_in")
         warm_out = keep.tile([P, 1], F32, name="warm_out")
 
         nc.vector.memset(table_scales[:].bitcast(I32), 0)
         nc.vector.memset(wk_planes[:].bitcast(I32), 0)
-        nc.vector.memset(wv4_plane[:].bitcast(I32), 0)
+        nc.vector.memset(staged[:, J:].bitcast(I32), 0)
         nc.vector.memset(warm_in[:], 0.0)
         nc.scalar.activation(warm_out[:], warm_in[:], SIGMOID)
 
@@ -83,15 +84,12 @@ def tile_list_engram_qf_sig_kernel(
                 wk_late[:].bitcast(I32), wk_words[:, :, N // 2 :, :].rearrange("a p n i -> p a (n i)").bitcast(I32)
             )
 
-        def load_wv4_scales(r):
-            nc.sync.dma_start(wv4_plane[r:P:32, :].bitcast(I32), wv4_scales[0, r:16:4, :].bitcast(I32))
-
         def load_table_scales(a):
             nc.sync.dma_start(table_scales[32 + 2 * (1 - a) : 96 : 4, :].bitcast(I32), tab_scales[a].bitcast(I32))
 
         def place_picked_scales(r):
             nc.sync.dma_start(
-                picked_planes[r:P:4, :].bitcast(I32), picked_scales[32 + 4 * r : 95 + 4 * r : 2, :].bitcast(I32)
+                picked_planes[r:P:4, :].bitcast(I32), staged[32 + 4 * r : 95 + 4 * r : 2, :].bitcast(I32)
             )
 
         def load_wk_scales(r):
@@ -112,18 +110,18 @@ def tile_list_engram_qf_sig_kernel(
         nc.sync.dma_start(offsets[:], offs)
         load_table_scales(0)
         load_table_scales(1)
+        nc.sync.dma_start(staged[32:96:4, J:].bitcast(I32), wv4_scales[0].bitcast(I32))
         load_table(0, halves[1])
         load_wk_early(0)
         for r in range(4):
             load_wk_scales(r)
         load_wv8(0)
-        load_table(1, halves[0])
+        load_table(1, slice(0, 3 * T // 8))
         nc.vector.tensor_copy(picked_scales[:], table_scales[:].indirect(offsets[:]))
+        nc.vector.tensor_copy(staged[:, :J].bitcast(I32), picked_scales[:].bitcast(I32))
         for r in range(4):
             place_picked_scales(r)
-        load_table(1, halves[1])
-        for r in range(4):
-            load_wv4_scales(r)
+        load_table(1, slice(3 * T // 8, T))
         load_wv8(1)
         load_wk_early(1)
         nc.sync.dma_start(st_sb[0][:, :HALF], st[:P, :HALF])

@@ -204,7 +204,9 @@ def tile_list_engram_qf_sig_kernel(
 
         gates = {}
 
-        keys = {(c, h): key(c, h) for h in range(HALVES) for c in range(2)}
+        keys = {t: key(*t) for t in ((0, 0), (1, 0), (0, 1))}
+        values = {(0, 0): value(0, 0)}
+        keys.update({(1, 1): key(1, 1)})
 
         def gate(c, h):
             ke = keys[(c, h)] if (c, h) in keys else key(c, h)
@@ -219,10 +221,12 @@ def tile_list_engram_qf_sig_kernel(
             gates.update({(c, h): opened})
 
         def product(c, h):
-            nc.vector.tensor_tensor(gated_tile(c, h), value(c, h)[:], gates[(c, h)], MULT)
+            nc.vector.tensor_tensor(gated_tile(c, h), (values[(c, h)] if (c, h) in values else value(c, h))[:], gates[(c, h)], MULT)
 
-        def add(engine, c, h):
-            engine.tensor_tensor(out_sb[c][:, columns(h)], gated_tile(c, h), res_sb[c][:, columns(h)], ADD)
+        def add(engine, c, h, part=slice(0, HALF)):
+            cols = slice(h * HALF + part.start, h * HALF + part.stop)
+            engine.tensor_tensor(out_sb[c][:, cols], gated_tile(c, h)[:, part], res_sb[c][:, cols], ADD)
+            return cols
 
         def store(c, cols):
             nc.sync.dma_start(out[c * P : (c + 1) * P, cols], out_sb[c][:, cols])
@@ -236,6 +240,10 @@ def tile_list_engram_qf_sig_kernel(
         product(CHUNKS - 1, 1)
         for t in range(CHUNKS * HALVES):
             c, h = divmod(t, HALVES)
+            if t >= GPSIMD_ADDS:
+                for part in (slice(0, HALF // 2), slice(HALF // 2, HALF)):
+                    store(c, add(nc.vector, c, h, part))
+                continue
             add(nc.gpsimd if t < GPSIMD_ADDS else nc.vector, c, h)
             if c >= CHUNKS // 2:
                 store(c, columns(h))

@@ -21,7 +21,8 @@ P = 128
 PACK = 4
 HALF = 512
 GPSIMD_ADDS = 5
-VALUE_BANKS = {(2, 0): 4, (2, 1): 0, (3, 0): 1, (3, 1): 7}
+KEY_BANKS = ((0, 1), (2, 3), (6, 7), (0, 3))
+VALUE_BANKS = ((4, 5), (1, 4), (2, 6), (7, 4))
 CHUNKS = N // P
 HALVES = J // HALF
 SCALE_ROW0 = (4, 0)
@@ -50,7 +51,7 @@ def tile_list_engram_qf_sig_kernel(
         st_sb = [keep.tile([P, J], F32, name="st%d" % c) for c in range(CHUNKS)]
         res_sb = [keep.tile([P, J], F32, name="res%d" % c) for c in range(CHUNKS)]
         out_all = keep.tile([P, CHUNKS * J], F32, name="out_all")
-        out_sb = [out_all[:, c * J : (c + 1) * J] for c in range(CHUNKS)]
+        out_sb = {c: out_all[:, c * J : (c + 1) * J] for c in range(1, CHUNKS)}
         gated = [keep.tile([P, J], F32, name="gated%d" % c) for c in range(CHUNKS)]
         picked_words = [
             [keep.tile([P, HALF], U32, name="picked%d_%d" % (a, h), align_bytes=64) for h in range(HALVES)]
@@ -115,18 +116,18 @@ def tile_list_engram_qf_sig_kernel(
         load_wk_early(0)
         for r in range(4):
             load_wk_scales(r)
-        load_wv8(0)
-        load_table(1, slice(0, 3 * T // 8))
+        load_table(1, slice(0, 5 * T // 8))
         nc.vector.tensor_copy(picked_scales[:], table_scales[:].indirect(offsets[:]))
         nc.vector.tensor_copy(staged[:, :J].bitcast(I32), picked_scales[:].bitcast(I32))
         for r in range(4):
             place_picked_scales(r)
-        load_table(1, slice(3 * T // 8, T))
-        load_wv8(1)
+        load_table(1, slice(5 * T // 8, T))
         load_wk_early(1)
-        nc.sync.dma_start(st_sb[0][:, :HALF], st[:P, :HALF])
+        load_wv8(0)
         nc.sync.dma_start(wv4_sb[:].bitcast(I32), wv4_words[0].bitcast(I32))
+        nc.sync.dma_start(st_sb[0][:, :HALF], st[:P, :HALF])
         nc.sync.dma_start(st_sb[0][:, HALF:], st[:P, HALF:])
+        load_wv8(1)
         for c in range(CHUNKS):
             if c + 1 < CHUNKS:
                 load_rows(st_sb, st, c + 1)
@@ -134,30 +135,36 @@ def tile_list_engram_qf_sig_kernel(
             if c == 0:
                 load_wk_late()
 
+        def interleave_wv8(u):
+            nc.scalar.copy(wv8_bf[u][:, :P, :], wv8_raw[u][:, :, :P].rearrange("p i n -> p n i"))
+            nc.gpsimd.tensor_scalar(
+                wv8_bf[u][:, P:, :], wv8_raw[u][:, :, P:].rearrange("p i n -> p n i"), 1.0, 0.0, MULT, ADD
+            )
+
         def quantise_wv8(u):
-            nc.scalar.copy(wv8_bf[u][:], wv8_raw[u][:].rearrange("p i n -> p n i"))
             nc.vector.quantize_mx(
                 out=wv8_codes[u][:].bitcast(FP8X4),
                 scales=wv8_plane[u][:],
                 in_=wv8_bf[u][:].rearrange("p n i -> p (n i)"),
             )
 
+        for u in range(2):
+            interleave_wv8(u)
+
         def gather(dst, window, h):
             nc.vector.tensor_copy(dst[:], window[:].indirect(offsets[:, h * HALF // 16 : (h + 1) * HALF // 16]))
 
         for h in range(HALVES):
             gather(picked_words[0][h], table[0], h)
-        quantise_wv8(0)
         for h in range(HALVES):
             gather(picked_words[1][h], table[1], h)
-        quantise_wv8(1)
 
         def picked(a, h):
             return dict(rhs=picked_words[a][h][:].bitcast(FP8X4), rhs_scale=picked_planes[SCALE_ROW0[a] : P, h * HALF : (h + 1) * HALF])
 
         def key(c, h):
             rows = slice(c * P, (c + 1) * P)
-            ke = psum.tile([P, HALF], F32, name="bank%d" % (2 * (c % 2) + h))
+            ke = psum.tile([P, HALF], F32, name="bank%d" % KEY_BANKS[c][h])
             within = slice(c % 2 * P, (c % 2 + 1) * P)
             for a in range(2):
                 words = wk_early[a][:, within] if c < 2 else wk_late[:, a, within]
@@ -171,26 +178,28 @@ def tile_list_engram_qf_sig_kernel(
                 )
             return ke
 
+        def open_value(c, h):
+            ve = psum.tile([P, HALF], F32, name="bank%d" % VALUE_BANKS[c][h])
+            nc.tensor.matmul_mx(
+                out=ve[:],
+                lhsT=wv4_sb[:, 2 * c * P : 2 * (c + 1) * P].bitcast(FP4X4),
+                lhsT_scale=wv4_plane[:, c * P : (c + 1) * P],
+                start=True,
+                stop=False,
+                **picked(1, h),
+            )
+            return ve
+
         def value(c, h):
-            rows = slice(c * P, (c + 1) * P)
             within = slice(c % 2 * P, (c % 2 + 1) * P)
-            b = 4 + 2 * c + h if c < 2 else VALUE_BANKS[(c, h)]
-            ve = psum.tile([P, HALF], F32, name="bank%d" % b)
+            ve = values[(c, h)] if c == 0 else open_value(c, h)
             nc.tensor.matmul_mx(
                 out=ve[:],
                 lhsT=wv8_codes[c // 2][:, within].bitcast(FP8X4),
                 lhsT_scale=wv8_plane[c // 2][:, within],
-                start=True,
-                stop=False,
-                **picked(0, h),
-            )
-            nc.tensor.matmul_mx(
-                out=ve[:],
-                lhsT=wv4_sb[:, 2 * c * P : 2 * (c + 1) * P].bitcast(FP4X4),
-                lhsT_scale=wv4_plane[:, rows],
                 start=False,
                 stop=True,
-                **picked(1, h),
+                **picked(0, h),
             )
             return ve
 
@@ -204,9 +213,8 @@ def tile_list_engram_qf_sig_kernel(
 
         gates = {}
 
-        keys = {t: key(*t) for t in ((0, 0), (1, 0), (0, 1))}
-        values = {(0, 0): value(0, 0)}
-        keys.update({(1, 1): key(1, 1)})
+        keys = {t: key(*t) for t in ((0, 0), (1, 0), (0, 1), (1, 1))}
+        values = {(0, h): open_value(0, h) for h in range(HALVES)}
 
         def gate(c, h):
             ke = keys[(c, h)] if (c, h) in keys else key(c, h)
@@ -215,13 +223,15 @@ def tile_list_engram_qf_sig_kernel(
             if c == CHUNKS - 1:
                 first = (GPSIMD_ADDS + h) * HALF
                 opened = out_all[:, first : first + HALF]
+            elif (c, h) == (0, 1):
+                opened = wv8_raw[1][:].rearrange("p i n -> p (i n)")[:, :HALF]
             else:
                 opened = work.tile([P, HALF], F32, name="opened")[:]
             nc.scalar.activation(opened, logit[:], SIGMOID)
             gates.update({(c, h): opened})
 
         def product(c, h):
-            nc.vector.tensor_tensor(gated_tile(c, h), (values[(c, h)] if (c, h) in values else value(c, h))[:], gates[(c, h)], MULT)
+            nc.vector.tensor_tensor(gated_tile(c, h), value(c, h)[:], gates[(c, h)], MULT)
 
         def add(engine, c, h, part=slice(0, HALF)):
             cols = slice(h * HALF + part.start, h * HALF + part.stop)
@@ -233,11 +243,15 @@ def tile_list_engram_qf_sig_kernel(
 
         for c in range(CHUNKS):
             gate(c, 0)
+            if c < 2:
+                quantise_wv8(c)
             gate(c, 1)
             if c > 0:
                 product(c - 1, 1)
             product(c, 0)
         product(CHUNKS - 1, 1)
+        out_first = keep.tile([P, J], F32, name="wv8_bf1", align_bytes=64)
+        out_sb.update({0: out_first[:]})
         for t in range(CHUNKS * HALVES):
             c, h = divmod(t, HALVES)
             if t >= GPSIMD_ADDS:

from contextlib import ExitStack

import concourse.mybir as mybir

K, N, T, J = 1024, 512, 4096, 1024
FLOPS = 2 * 2 * K * N * J

F32 = mybir.dt.float32
BF16 = mybir.dt.bfloat16
I32 = mybir.dt.int32
U32 = mybir.dt.uint32
U16 = mybir.dt.uint16
U8 = mybir.dt.uint8
FP8X4 = mybir.dt.float8_e4m3fn_x4
FP4X4 = mybir.dt.float4_e2m1fn_x4
MULT = mybir.AluOpType.mult
ADD = mybir.AluOpType.add
SIGMOID = mybir.ActivationFunctionType.Sigmoid

P = 128
PACK = 4
HALF = 512
GPSIMD_ADDS = 5
KEY_BANKS = ((0, 1), (2, 3), (6, 7), (0, 3))
VALUE_BANKS = ((4, 5), (1, 4), (2, 6), (7, 4))
CHUNKS = N // P
HALVES = J // HALF
SCALE_ROW0 = (4, 0)


def tile_list_engram_qf_sig_kernel(
    tc, tab_words, tab_scales, wk_words, wk_scales, wv8, wv4_words, wv4_scales, st, res, offs, out
):
    nc = tc.nc
    with ExitStack() as ctx:
        keep = ctx.enter_context(tc.tile_pool(name="keep", bufs=1))
        work = ctx.enter_context(tc.tile_pool(name="work", bufs=4))
        psum = ctx.enter_context(tc.psum_pool(name="psum", bufs=1))

        offsets = keep.tile([P, J // 16], U16, name="offsets")
        table = [keep.tile([P, T], U32, name="table%d" % a, align_bytes=64) for a in range(2)]
        table_scales = keep.tile([P, T], U8, name="table_scales", align_bytes=64)
        wk_planes = keep.tile([P, 2, N], U8, name="wk_planes", align_bytes=64)
        wk_early = [keep.tile([P, N // 2], U32, name="wk_early%d" % a, align_bytes=64) for a in range(2)]
        wk_late = keep.tile([P, 2, N // 2], U32, name="wk_late", align_bytes=64)
        wv4_sb = keep.tile([P, 2 * N], U8, name="wv4_sb", align_bytes=64)
        wv8_raw = [keep.tile([P, PACK, N // 2], F32, name="wv8_raw%d" % u, align_bytes=64) for u in range(2)]
        wv8_bf = [keep.tile([P, N // 2, PACK], BF16, name="wv8_bf%d" % u, align_bytes=64) for u in range(2)]
        wv8_codes = [keep.tile([P, N // 2], U32, name="wv8_codes%d" % u, align_bytes=64) for u in range(2)]
        wv8_plane = [keep.tile([P, N // 2], U8, name="wv8_plane%d" % u, align_bytes=64) for u in range(2)]
        st_sb = [keep.tile([P, J], F32, name="st%d" % c) for c in range(CHUNKS)]
        res_sb = [keep.tile([P, J], F32, name="res%d" % c) for c in range(CHUNKS)]
        out_all = keep.tile([P, CHUNKS * J], F32, name="out_all")
        out_sb = {c: out_all[:, c * J : (c + 1) * J] for c in range(1, CHUNKS)}
        gated = [keep.tile([P, J], F32, name="gated%d" % c) for c in range(CHUNKS)]
        picked_words = [
            [keep.tile([P, HALF], U32, name="picked%d_%d" % (a, h), align_bytes=64) for h in range(HALVES)]
            for a in range(2)
        ]
        picked_scales = keep.tile([P, J], U8, name="picked_scales", align_bytes=64)
        staged = keep.tile([P, J + N], U8, name="staged", align_bytes=64)
        picked_planes = keep.tile([P, J + N], U8, name="picked_planes", align_bytes=64)
        wv4_plane = picked_planes[:, J:]
        warm_in = keep.tile([P, 1], F32, name="warm_in")
        warm_out = keep.tile([P, 1], F32, name="warm_out")

        nc.vector.memset(table_scales[:].bitcast(I32), 0)
        nc.vector.memset(wk_planes[:].bitcast(I32), 0)
        nc.vector.memset(staged[:, J:].bitcast(I32), 0)
        nc.vector.memset(warm_in[:], 0.0)
        nc.scalar.activation(warm_out[:], warm_in[:], SIGMOID)

        def load_table(a, cols):
            nc.sync.dma_start(
                table[a][:, cols].bitcast(I32), tab_words[a, :, cols, :].rearrange("p t i -> p (t i)").bitcast(I32)
            )

        def load_wk_early(a):
            nc.sync.dma_start(
                wk_early[a][:].bitcast(I32), wk_words[a, :, : N // 2, :].rearrange("p n i -> p (n i)").bitcast(I32)
            )

        def load_wk_late():
            nc.sync.dma_start(
                wk_late[:].bitcast(I32), wk_words[:, :, N // 2 :, :].rearrange("a p n i -> p a (n i)").bitcast(I32)
            )

        def load_table_scales(a):
            nc.sync.dma_start(table_scales[32 + 2 * (1 - a) : 96 : 4, :].bitcast(I32), tab_scales[a].bitcast(I32))

        def place_picked_scales(r):
            nc.sync.dma_start(
                picked_planes[r:P:4, :].bitcast(I32), staged[32 + 4 * r : 95 + 4 * r : 2, :].bitcast(I32)
            )

        def load_wk_scales(r):
            nc.sync.dma_start(
                wk_planes[r:P:32, :, :].bitcast(I32),
                wk_scales[:, r:16:4, :].rearrange("a q n -> q a n").bitcast(I32),
            )

        def load_wv8(u):
            cols = slice(u * N // 2, (u + 1) * N // 2)
            nc.sync.dma_start(wv8_raw[u][:], wv8[:, cols].rearrange("(p i) n -> p i n", i=PACK))

        def load_rows(tiles, source, c):
            nc.sync.dma_start(tiles[c][:], source[c * P : (c + 1) * P, :])

        halves = (slice(0, T // 2), slice(T // 2, T))
        load_table(0, halves[0])
        nc.sync.dma_start(offsets[:], offs)
        load_table_scales(0)
        load_table_scales(1)
        nc.sync.dma_start(staged[32:96:4, J:].bitcast(I32), wv4_scales[0].bitcast(I32))
        load_table(0, halves[1])
        load_wk_early(0)
        for r in range(4):
            load_wk_scales(r)
        load_table(1, slice(0, 5 * T // 8))
        nc.vector.tensor_copy(picked_scales[:], table_scales[:].indirect(offsets[:]))
        nc.vector.tensor_copy(staged[:, :J].bitcast(I32), picked_scales[:].bitcast(I32))
        for r in range(4):
            place_picked_scales(r)
        load_table(1, slice(5 * T // 8, T))
        load_wk_early(1)
        load_wv8(0)
        nc.sync.dma_start(wv4_sb[:].bitcast(I32), wv4_words[0].bitcast(I32))
        nc.sync.dma_start(st_sb[0][:, :HALF], st[:P, :HALF])
        nc.sync.dma_start(st_sb[0][:, HALF:], st[:P, HALF:])
        load_wv8(1)
        for c in range(CHUNKS):
            if c + 1 < CHUNKS:
                load_rows(st_sb, st, c + 1)
            load_rows(res_sb, res, c)
            if c == 0:
                load_wk_late()

        def interleave_wv8(u):
            nc.scalar.copy(wv8_bf[u][:, :P, :], wv8_raw[u][:, :, :P].rearrange("p i n -> p n i"))
            nc.gpsimd.tensor_scalar(
                wv8_bf[u][:, P:, :], wv8_raw[u][:, :, P:].rearrange("p i n -> p n i"), 1.0, 0.0, MULT, ADD
            )

        def quantise_wv8(u):
            nc.vector.quantize_mx(
                out=wv8_codes[u][:].bitcast(FP8X4),
                scales=wv8_plane[u][:],
                in_=wv8_bf[u][:].rearrange("p n i -> p (n i)"),
            )

        for u in range(2):
            interleave_wv8(u)

        def gather(dst, window, h):
            nc.vector.tensor_copy(dst[:], window[:].indirect(offsets[:, h * HALF // 16 : (h + 1) * HALF // 16]))

        for h in range(HALVES):
            gather(picked_words[0][h], table[0], h)
        for h in range(HALVES):
            gather(picked_words[1][h], table[1], h)

        def picked(a, h):
            return dict(rhs=picked_words[a][h][:].bitcast(FP8X4), rhs_scale=picked_planes[SCALE_ROW0[a] : P, h * HALF : (h + 1) * HALF])

        def key(c, h):
            rows = slice(c * P, (c + 1) * P)
            ke = psum.tile([P, HALF], F32, name="bank%d" % KEY_BANKS[c][h])
            within = slice(c % 2 * P, (c % 2 + 1) * P)
            for a in range(2):
                words = wk_early[a][:, within] if c < 2 else wk_late[:, a, within]
                nc.tensor.matmul_mx(
                    out=ke[:],
                    lhsT=words.bitcast(FP8X4),
                    lhsT_scale=wk_planes[:, a, rows],
                    start=(a == 0),
                    stop=(a == 1),
                    **picked(a, h),
                )
            return ke

        def open_value(c, h):
            ve = psum.tile([P, HALF], F32, name="bank%d" % VALUE_BANKS[c][h])
            nc.tensor.matmul_mx(
                out=ve[:],
                lhsT=wv4_sb[:, 2 * c * P : 2 * (c + 1) * P].bitcast(FP4X4),
                lhsT_scale=wv4_plane[:, c * P : (c + 1) * P],
                start=True,
                stop=False,
                **picked(1, h),
            )
            return ve

        def value(c, h):
            within = slice(c % 2 * P, (c % 2 + 1) * P)
            ve = values[(c, h)] if c == 0 else open_value(c, h)
            nc.tensor.matmul_mx(
                out=ve[:],
                lhsT=wv8_codes[c // 2][:, within].bitcast(FP8X4),
                lhsT_scale=wv8_plane[c // 2][:, within],
                start=False,
                stop=True,
                **picked(0, h),
            )
            return ve

        def columns(h):
            return slice(h * HALF, (h + 1) * HALF)

        def gated_tile(c, h):
            if h == 1 and c < CHUNKS - 1:
                return st_sb[c + 1][:, :HALF]
            return gated[c][:, columns(h)]

        gates = {}

        keys = {t: key(*t) for t in ((0, 0), (1, 0), (0, 1), (1, 1))}
        values = {(0, h): open_value(0, h) for h in range(HALVES)}

        def gate(c, h):
            ke = keys[(c, h)] if (c, h) in keys else key(c, h)
            logit = work.tile([P, HALF], F32, name="logit")
            nc.vector.tensor_tensor(logit[:], ke[:], st_sb[c][:, columns(h)], MULT)
            if c == CHUNKS - 1:
                first = (GPSIMD_ADDS + h) * HALF
                opened = out_all[:, first : first + HALF]
            elif (c, h) == (0, 1):
                opened = wv8_raw[1][:].rearrange("p i n -> p (i n)")[:, :HALF]
            else:
                opened = work.tile([P, HALF], F32, name="opened")[:]
            nc.scalar.activation(opened, logit[:], SIGMOID)
            gates.update({(c, h): opened})

        def product(c, h):
            nc.vector.tensor_tensor(gated_tile(c, h), value(c, h)[:], gates[(c, h)], MULT)

        def add(engine, c, h, part=slice(0, HALF)):
            cols = slice(h * HALF + part.start, h * HALF + part.stop)
            engine.tensor_tensor(out_sb[c][:, cols], gated_tile(c, h)[:, part], res_sb[c][:, cols], ADD)
            return cols

        def store(c, cols):
            nc.sync.dma_start(out[c * P : (c + 1) * P, cols], out_sb[c][:, cols])

        for c in range(CHUNKS):
            gate(c, 0)
            if c < 2:
                quantise_wv8(c)
            gate(c, 1)
            if c > 0:
                product(c - 1, 1)
            product(c, 0)
        product(CHUNKS - 1, 1)
        out_first = keep.tile([P, J], F32, name="wv8_bf1", align_bytes=64)
        out_sb.update({0: out_first[:]})
        for t in range(CHUNKS * HALVES):
            c, h = divmod(t, HALVES)
            if t >= GPSIMD_ADDS:
                for part in (slice(0, HALF // 2), slice(HALF // 2, HALF)):
                    store(c, add(nc.vector, c, h, part))
                continue
            add(nc.gpsimd if t < GPSIMD_ADDS else nc.vector, c, h)
            if c >= CHUNKS // 2:
                store(c, columns(h))
            elif h == 1:
                store(c, slice(0, J))
